import numpy as np, ml_dtypes
CORES = [56,61,80,85]
N = 4
import mx_ref
NC, G = 128, 2
C, C2 = np.float32(0.031), np.float32(0.0155)
BF = ml_dtypes.bfloat16
def cut(t, i, w=512):
    return t[:, w * i:w * i + w]
def tile(rs):
    return np.stack(rs, axis=2).reshape(128, -1).astype(BF)
def layer(w, X):
    out = []
    for i in range(G):
        for t in range(len(X)):
            p = mx_ref.matmul(mx_ref.quantize(cut(w, len(X) * i + t)), X[t])
            z = p if t == 0 else z + p
        out.append(z)
    return out
def act(Z):
    return [np.maximum(s * z, 0) * C for z in Z for s in (1, -1)]
def act2(Z):
    return [np.maximum(s * z, 0) * C2 for z in Z for s in (1, -1)]
def setup_inputs(rng):
    def f(*shape):
        return mx_ref.flush((rng.standard_normal(shape, dtype=np.float32) * np.exp2(rng.integers(-2, 3, shape[:-1] + (1,)))).astype(BF))
    return {"x": f(N, 128, 4 * NC), "w1": f(N, 128, G * 512), "w2": f(N, 128, G * 512), "w3": f(N, 128, G * 512), "w4": f(N, 128, 512)}
def setup_inputs_blocks(rng):
    d = setup_inputs(rng)
    for k in ("x", "w1", "w2", "w3", "w4"): d[k] = mx_ref.spread(d[k], rng, 2)
    return d
def setup_inputs_wide(rng):
    d = setup_inputs(rng)
    for k in ("x", "w1", "w2", "w3", "w4"): d[k] = mx_ref.flush((d[k].astype(np.float32) * np.exp2(rng.integers(-4, 5, (N, 1, 1))).astype(np.float32)).astype(BF))
    return d
def reference(x, w1, w2, w3, w4, own=None):
    X = [mx_ref.quantize(x[j]) for j in range(N)]
    t = np.stack([np.stack([tile(act(layer(w1[r], [X[c]]))) for c in range(N)]) for r in range(N)])
    uset = t if own is None else own["t"]
    h = np.zeros((N, 128, 4 * NC), BF)
    for c in range(N):
        for r in range(N):
            P = layer(w2[r], [mx_ref.quantize(uset[r][c])])
            Z = P if r == 0 else [z + p for z, p in zip(Z, P)]
        h[c] = tile(act2(Z))
    use = h if own is None else own["h"]
    H = [mx_ref.quantize(use[j]) for j in range(N)]
    y = np.zeros((N, 128, NC), np.float32)
    for c in range(N):
        for r in range(N):
            p = mx_ref.matmul(mx_ref.quantize(w4[r]), mx_ref.quantize(tile(act(layer(w3[r], [H[c]])))))
            y[c] = p if r == 0 else y[c] + p
    return {"t": t, "h": h, "y": y}

@@ -1,0 +1,341 @@
+from concourse.bass import DstId, RemoteDMATransfer
+from concourse.mybir import dt, AluOpType, ActivationFunctionType
+
+SIM_CORES = 96
+C1, C2 = 0.031, 0.0155
+F8, U8, BF, F32 = "float8_e4m3fn_x4", "uint8", "bfloat16", "float32"
+
+SCRATCH = {
+    "xin": ("sbuf", [128, 512], BF), "w1in": ("sbuf", [128, 1024], BF), "w2in": ("sbuf", [128, 1024], BF),
+    "w34in": ("sbuf", [128, 1536], BF),
+    "xq": ("sbuf", [128, 128], F8), "xs": ("sbuf", [128, 128], U8),
+    "xpq": ("sbuf", [128, 128], F8), "xps": ("sbuf", [128, 128], U8),
+    "xrq": ("sbuf", [128, 256], F8), "xrs": ("sbuf", [128, 256], U8),
+    "w1q": ("sbuf", [128, 256], F8), "w1s": ("sbuf", [128, 256], U8),
+    "w2q": ("sbuf", [128, 256], F8), "w2s": ("sbuf", [128, 256], U8),
+    "woq": ("sbuf", [128, 384], F8), "wos": ("sbuf", [128, 384], U8),
+    "wpq": ("sbuf", [128, 384], F8), "wps": ("sbuf", [128, 384], U8),
+    "w0q": ("sbuf", [128, 384], F8), "w0s": ("sbuf", [128, 384], U8),
+    "w1rq": ("sbuf", [128, 384], F8), "w1rs": ("sbuf", [128, 384], U8),
+    "to": ("sbuf", [128, 512], BF), "tp": ("sbuf", [128, 512], BF), "ta": ("sbuf", [128, 512], BF), "tb": ("sbuf", [128, 512], BF),
+    "tq": ("sbuf", [128, 512], F8), "ts": ("sbuf", [128, 512], U8),
+    "ht": ("sbuf", [128, 512], BF), "hq": ("sbuf", [128, 128], F8), "hs": ("sbuf", [128, 128], U8),
+    "ut": ("sbuf", [128, 2048], BF), "uq": ("sbuf", [128, 512], F8), "us": ("sbuf", [128, 512], U8),
+    "pp": ("sbuf", [128, 256], F32), "pr": ("sbuf", [128, 512], F32),
+    "pd": ("sbuf", [128, 128], F32), "arr": ("sbuf", [128, 256], F32),
+    "a0": ("sbuf", [128, 128], F32), "sm": ("sbuf", [128, 256], F32), "yo": ("sbuf", [128, 128], F32),
+    "rxq": ("sbuf", [128, 256], F8), "rxs": ("sbuf", [128, 256], U8),
+    "rwq": ("sbuf", [128, 384], F8), "rws": ("sbuf", [128, 384], U8),
+    "pin": ("sbuf", [128, 384], F32), "pf": ("sbuf", [128, 128], F32),
+}
+for _b in range(8):
+    SCRATCH["b%d" % _b] = ("psum", [128, 512], F32)
+
+SEMAPHORES = (["ld_x", "ld_w1", "ld_w2", "ld_w34", "st"]
+              + ["lx", "lw", "lpp", "lpr", "lrel"]
+              + ["xin_", "xr_", "wp_", "wr0_", "wr1_", "wc_", "ws_", "pd_", "pf_", "pin_", "s0_", "s1_"]
+              + ["q_x", "q_w1", "q_w2", "q_w34", "q_h"]
+              + [a + k for k in "opab" for a in ("z0", "z1", "act", "q_t", "y0", "y1", "act_u", "q_u")]
+              + ["m_po", "m_pp0", "m_pp1", "m_pa0", "m_pa1", "m_pb0", "m_pb1", "cp", "cr", "a0d", "s0d", "s1d", "act_h", "m_y", "y_c"])
+
+
+def plan(T, topo):
+    cores = list(T.cores)
+    chips = sorted({topo.chip(c) for c in cores})
+    everyone = range(SIM_CORES)
+    on = {ch: [c for c in cores if topo.chip(c) == ch] for ch in chips}
+    far = {c: [d for d in cores if topo.chip(d) != topo.chip(c)] for c in cores}
+    mate_of = {c: [d for d in on[topo.chip(c)] if d != c][0] for c in cores}
+
+    def owners(ch, die, dst):
+        return [c for c in everyone if c not in cores and topo.chip(c) == ch and topo.die(c) == die and topo.may_write(c, dst)]
+    lane = {}
+    for d in cores:
+        lane[d] = owners(topo.chip(far[d][0]), topo.die(d), d)[:2]
+    fwd = {}
+    for s in cores:
+        fwd[s] = owners(topo.chip(s), topo.die(s), far[s][0])[1]
+    wrel = {}
+    for s in cores:
+        fc = topo.chip(far[s][0])
+        ch = [m for m in sorted({topo.chip(c) for c in everyone}) if topo.mates(m, fc) and topo.same_plane(m, topo.chip(s))][0]
+        wrel[s] = owners(ch, topo.die(s), far[s][0])[0]
+    return cores, on, far, mate_of, lane, fwd, wrel
+
+
+def rank_program(g, core, T, topo):
+    cores, on, far, mate_of, lane, fwd, wrel = plan(T, topo)
+    S = T.sem
+
+    def u8(ap):
+        return ap.bitcast(dt.uint8)
+
+    def bits(m):
+        return [1 << i for i in range(m.bit_length()) if (m >> i) & 1]
+
+    def transfer(srcs, dsts, mask, sem):
+        ids = []
+        for c, _ in dsts:
+            rid, pid, _se = topo.addr(c)
+            ids.append(DstId(rid=rid, pnc=pid))
+        return RemoteDMATransfer(dst_ids=ids, srcs=srcs, dsts=[ap for _, ap in dsts], dma_engine_mask=mask,
+                                 remote_sem=sem, alu_op=1 if len(srcs) > 1 else 0)
+
+    def send(trs, local_sem):
+        g.remote_dma_fused(trs, local_sem=local_sem)
+
+    if core not in cores:
+        relay(g, core, T, topo, S, transfer, send, u8)
+        return
+
+    rank = T.rank_of(core)
+    mate = mate_of[core]
+    k = on[topo.chip(core)].index(core)
+    fa, fb = far[core]
+    V, A, P, Y = g.vector, g.scalar, g.tensor, g.sync
+
+    Y.dma_start(T.xin[:], T.x[:]).then_inc(S.ld_x, 16)
+    A.dma_start(T.w1in[:], T.w1[:]).then_inc(S.ld_w1, 16)
+    Y.dma_start(T.w34in[:, 0:1024], T.w3[:]).then_inc(S.ld_w34, 16)
+    A.dma_start(T.w34in[:, 1024:1536], T.w4[:]).then_inc(S.ld_w34, 16)
+    Y.dma_start(T.w2in[:], T.w2[:]).then_inc(S.ld_w2, 16)
+
+    near = topo.mask(core, mate)
+    nb = bits(near)
+    off = topo.mask(core, wrel[core])
+    sl = slice(128 * k, 128 * k + 128)
+    g.wait_ge(S.q_x, 1)
+    send([transfer([u8(T.xq[:])], [(lane[d][0], u8(T.rxq[:, sl])) for d in (fa, fb)] + [(mate, u8(T.xpq[:]))], near, S.xin_)], S.lx)
+    send([transfer([T.xs[:]], [(lane[d][1], T.rxs[:, sl]) for d in (fa, fb)] + [(mate, T.xps[:])], near, S.xin_)], S.lx)
+    g.wait_ge(S.q_w34, 1)
+    send([transfer([u8(T.woq[:])], [(wrel[core], u8(T.rwq[:]))], off, S.wc_),
+          transfer([u8(T.woq[:])], [(mate, u8(T.wpq[:]))], near & ~off, S.wp_)], S.lw)
+    send([transfer([T.wos[:]], [(wrel[core], T.rws[:])], off, S.ws_),
+          transfer([T.wos[:]], [(mate, T.wps[:])], near & ~off, S.wp_)], S.lw)
+    g.wait_ge(S.cp, 2)
+    send([transfer([T.pp[:, 0:128]], [(mate, T.pd[:])], sum(nb[0::2]), S.pd_),
+          transfer([T.pp[:, 128:256]], [(fwd[core], T.pf[:])], sum(nb[1::2]), S.pf_)], S.lpp)
+    g.wait_ge(S.cr, 4)
+    trs = []
+    for i in (0, 1):
+        for n, d in enumerate((fa, fb)):
+            trs.append(transfer([T.pr[:, 256 * n + 128 * i:256 * n + 128 * i + 128]], [(lane[d][i], T.pin[:, sl])],
+                                sum(nb[2 * i + n::4]), S.pin_))
+    send(trs, S.lpr)
+    g.wait_ge(S.lx, 2 * len(nb))
+    g.wait_ge(S.lw, 2 * len(nb))
+    g.wait_ge(S.lpp, len(nb))
+    g.wait_ge(S.lpr, len(nb))
+
+    def vact(t, z, b, c, sem, n):
+        V.tensor_scalar(t[0][:, t[1] + b:t[1] + 512:4], z, 0.0, c, AluOpType.max, AluOpType.mult).then_inc(sem, 1)
+        V.tensor_scalar(t[0][:, t[1] + b + 1:t[1] + 512:4], z, 0.0, -c, AluOpType.min, AluOpType.mult).then_inc(sem, 1)
+
+    def sact(t, z, b, c, sem, n):
+        A.activation(t[0][:, t[1] + b:t[1] + 512:4], z, ActivationFunctionType.Relu, scale=c).then_inc(sem, 1)
+        A.activation(t[0][:, t[1] + b + 1:t[1] + 512:4], z, ActivationFunctionType.Relu, scale=-c).then_inc(sem, 1)
+
+    tiles = {"o": (T.to, 0), "p": (T.tp, 0), "a": (T.ta, 0), "b": (T.tb, 0)}
+    col = {"o": 0, "p": 128, "a": 256, "b": 384}
+    zb = {"o": (T.b0, T.b1), "p": (T.b4, T.b5), "a": (T.b0, T.b1), "b": (T.b4, T.b5)}
+    pb = {"o": (T.b2, T.b3), "p": (T.b6, T.b7), "a": (T.b0, T.b1), "b": (T.b4, T.b5)}
+    ub = {"o": (T.b6, T.b7), "p": (T.b0, T.b1), "a": (T.b4, T.b5), "b": (T.b2, T.b3)}
+    xin = {"o": (T.xq[:], T.xs[:]), "p": (T.xpq[:], T.xps[:]),
+           "a": (T.xrq[:, 0:128], T.xrs[:, 0:128]), "b": (T.xrq[:, 128:256], T.xrs[:, 128:256])}
+    wg = {"o": (T.woq, T.wos), "p": (T.wpq, T.wps), "a": (T.w0q, T.w0s), "b": (T.w1rq, T.w1rs)}
+
+    def w_t(q, s, i):
+        return q[:, 128 * i:128 * i + 128], s[:, 128 * i:128 * i + 128]
+
+    def mm(out, w, x, sem, start=True, stop=True):
+        ins = P.matmul_mx(out[:, 0:128], w[0], w[1], x[0], x[1], start, stop)
+        if sem is not None:
+            ins.then_inc(sem, 1)
+
+    def tcodes(c):
+        return T.tq[:, col[c]:col[c] + 128], T.ts[:, col[c]:col[c] + 128]
+
+    def ucodes(c):
+        return T.uq[:, col[c]:col[c] + 128], T.us[:, col[c]:col[c] + 128]
+
+    P.wait_ge(S.q_x, 1)
+    P.wait_ge(S.q_w1, 1)
+    for i in (0, 1):
+        mm(zb["o"][i], w_t(T.w1q, T.w1s, i), xin["o"], S["z%do" % i])
+    P.wait_ge(S.q_w2, 1)
+    P.wait_ge(S.q_to, 1)
+    for i in (0, 1):
+        mm(pb["o"][i], w_t(T.w2q, T.w2s, i), tcodes("o"), S.m_po)
+    P.wait_ge(S.xin_, 2 * len(nb))
+    for i in (0, 1):
+        mm(zb["p"][i], w_t(T.w1q, T.w1s, i), xin["p"], S["z%dp" % i])
+    P.wait_ge(S.q_tp, 1)
+    for i in (0, 1):
+        mm(pb["p"][i], w_t(T.w2q, T.w2s, i), tcodes("p"), S["m_pp%d" % i])
+    offn = len(bits(off))
+    P.wait_ge(S.xr_, 2 * offn)
+    for c in "ab":
+        for i in (0, 1):
+            mm(zb[c][i], w_t(T.w1q, T.w1s, i), xin[c], S["z%d%s" % (i, c)])
+    for c in "ab":
+        P.wait_ge(S["q_t" + c], 1)
+        for i in (0, 1):
+            mm(pb[c][i], w_t(T.w2q, T.w2s, i), tcodes(c), S["m_p%s%d" % (c, i)])
+    P.wait_ge(S.cp, 2)
+    P.wait_ge(S.cr, 4)
+    P.wait_ge(S.q_h, 1)
+    for c in "opab":
+        if c == "p":
+            P.wait_ge(S.wp_, 2 * (len(nb) - offn))
+        if c in "ab":
+            P.wait_ge(S["wr%d_" % "ab".index(c)], 2 * offn)
+        for i in (0, 1):
+            mm(ub[c][i], w_t(wg[c][0], wg[c][1], i), (T.hq[:], T.hs[:]), S["y%d%s" % (i, c)])
+    for c in "opab":
+        P.wait_ge(S["q_u" + c], 1)
+        mm(T.b6, w_t(wg[c][0], wg[c][1], 2), ucodes(c), S.m_y if c == "b" else None, c == "o", c == "b")
+
+    def quant(dst, src, sem):
+        V.quantize_mx(dst[0], dst[1], src).then_inc(sem, 1)
+
+    def vtile(c):
+        V.wait_ge(S["z0" + c], 1)
+        vact(tiles[c], zb[c][0][:, 0:128], 0, C1, S["act" + c], 2)
+
+    def vquant(c):
+        V.wait_ge(S["act" + c], 4)
+        quant(tcodes(c), tiles[c][0][:], S["q_t" + c])
+
+    V.wait_ge(S.ld_x, 16)
+    quant((T.xq[:], T.xs[:]), T.xin[:], S.q_x)
+    V.wait_ge(S.ld_w1, 16)
+    quant((T.w1q[:], T.w1s[:]), T.w1in[:], S.q_w1)
+    V.wait_ge(S.ld_w34, 32)
+    quant((T.woq[:], T.wos[:]), T.w34in[:], S.q_w34)
+    vtile("o")
+    vquant("o")
+    V.wait_ge(S.ld_w2, 16)
+    quant((T.w2q[:], T.w2s[:]), T.w2in[:], S.q_w2)
+    vtile("p")
+    vquant("p")
+    V.wait_ge(S.m_pp0, 1)
+    V.tensor_copy(T.pp[:, 0:128], pb["p"][0][:, 0:128]).then_inc(S.cp, 1)
+    vtile("a")
+    vtile("b")
+    vquant("a")
+    vquant("b")
+    for i in (0, 1):
+        V.wait_ge(S["m_pb%d" % i], 1)
+        V.tensor_copy(T.pr[:, 256 + 128 * i:384 + 128 * i], pb["b"][i][:, 0:128]).then_inc(S.cr, 1)
+    V.wait_ge(S.m_po, 2)
+    V.wait_ge(S.pd_, len(nb) // 2)
+    V.tensor_tensor(T.a0[:], pb["o"][0][:, 0:128], T.pd[:], AluOpType.add).then_inc(S.a0d, 1)
+    V.wait_ge(S.a0d, 1)
+    V.wait_ge(S.s0_, offn)
+    V.tensor_tensor(T.sm[:, 0:128], T.a0[:], T.arr[:, 0:128], AluOpType.add).then_inc(S.s0d, 1)
+    V.wait_ge(S.s1_, offn)
+    V.tensor_tensor(T.sm[:, 128:256], pb["o"][1][:, 0:128], T.arr[:, 128:256], AluOpType.add).then_inc(S.s1d, 1)
+    V.wait_ge(S.s0d, 1)
+    vact((T.ht, 0), T.sm[:, 0:128], 0, C2, S.act_h, 2)
+    V.wait_ge(S.act_h, 4)
+    quant((T.hq[:], T.hs[:]), T.ht[:], S.q_h)
+
+    def vu(c):
+        V.wait_ge(S["y0" + c], 1)
+        vact((T.ut, 4 * col[c]), ub[c][0][:, 0:128], 0, C1, S["act_u" + c], 2)
+
+    def vuq(c):
+        V.wait_ge(S["act_u" + c], 4)
+        quant(ucodes(c), T.ut[:, 4 * col[c]:4 * col[c] + 512], S["q_u" + c])
+    vu("o")
+    vu("p")
+    vuq("o")
+    vu("a")
+    vuq("p")
+    vu("b")
+    vuq("a")
+    vuq("b")
+    V.wait_ge(S.m_y, 1)
+    V.tensor_copy(T.yo[:], T.b6[:, 0:128]).then_inc(S.y_c, 1)
+
+    def stile(c):
+        A.wait_ge(S["z1" + c], 1)
+        sact(tiles[c], zb[c][1][:, 0:128], 2, C1, S["act" + c], 2)
+    stile("o")
+    stile("p")
+    A.wait_ge(S.m_pp1, 1)
+    A.activation(T.pp[:, 128:256], pb["p"][1][:, 0:128], ActivationFunctionType.Copy).then_inc(S.cp, 1)
+    stile("a")
+    stile("b")
+    for i in (0, 1):
+        A.wait_ge(S["m_pa%d" % i], 1)
+        A.activation(T.pr[:, 128 * i:128 * i + 128], pb["a"][i][:, 0:128], ActivationFunctionType.Copy).then_inc(S.cr, 1)
+    A.wait_ge(S.s1d, 1)
+    sact((T.ht, 0), T.sm[:, 128:256], 2, C2, S.act_h, 2)
+    for c in "opab":
+        A.wait_ge(S["y1" + c], 1)
+        sact((T.ut, 4 * col[c]), ub[c][1][:, 0:128], 2, C1, S["act_u" + c], 2)
+
+    Y.wait_ge(S.lw, 2 * len(nb))
+    for c, d in (("o", core), ("p", mate)):
+        Y.wait_ge(S["act" + c], 4)
+        Y.dma_start(T.t[T.rank_of(d)], tiles[c][0][:]).then_inc(S.st, 16)
+    Y.wait_ge(S.lpr, len(nb))
+    for c, d in (("a", fa), ("b", fb)):
+        Y.wait_ge(S["act" + c], 4)
+        Y.dma_start(T.t[T.rank_of(d)], tiles[c][0][:]).then_inc(S.st, 16)
+    Y.wait_ge(S.act_h, 4)
+    Y.dma_start(T.h[:], T.ht[:]).then_inc(S.st, 16)
+    Y.wait_ge(S.y_c, 1)
+    Y.dma_start(T.y[:], T.yo[:]).then_inc(S.st, 16)
+    Y.wait_ge(S.st, 96)
+
+
+def relay(g, core, T, topo, S, transfer, send, u8):
+    cores, on, far, mate_of, lane, fwd, wrel = plan(T, topo)
+    sent = [0]
+
+    def count(m):
+        return sum((m >> i) & 1 for i in range(m.bit_length()))
+
+    for s in cores:
+        if wrel[s] == core:
+            k = on[topo.chip(s)].index(s)
+            m = topo.mask(core, far[s][0])
+            n = count(topo.mask(s, core))
+            q, p, sem = (T.w0q, T.w0s, S.wr0_) if k == 0 else (T.w1rq, T.w1rs, S.wr1_)
+            g.wait_ge(S.wc_, n)
+            send([transfer([u8(T.rwq[:])], [(d, u8(q[:])) for d in far[s]], m, sem)], S.lrel)
+            g.wait_ge(S.ws_, n)
+            send([transfer([T.rws[:]], [(d, p[:]) for d in far[s]], m, sem)], S.lrel)
+            sent[0] += 2 * count(m)
+    for d in cores:
+        if core not in lane[d]:
+            continue
+        i = lane[d].index(core)
+        srcs = far[d]
+        m = topo.mask(core, d)
+        near = count(topo.mask(srcs[0], core))
+        g.wait_ge(S.xin_, 2 * near)
+        if i == 0:
+            send([transfer([u8(T.rxq[:])], [(d, u8(T.xrq[:]))], m, S.xr_)], S.lrel)
+        else:
+            send([transfer([T.rxs[:]], [(d, T.xrs[:])], m, S.xr_)], S.lrel)
+        sent[0] += count(m)
+        extra = 0
+        for s in srcs:
+            if fwd[s] == core:
+                to = lane[mate_of[s]][1]
+                g.wait_ge(S.pf_, near // 2)
+                mm = topo.mask(core, to)
+                send([transfer([T.pf[:]], [(to, T.pin[:, 256:384])], mm, S.pin_)], S.lrel)
+                sent[0] += count(mm)
+        if i == 1:
+            s = mate_of[d]
+            extra = count(topo.mask(fwd[s], core))
+        g.wait_ge(S.pin_, near // 2 + extra)
+        parts = [T.pin[:, 128 * j:128 * j + 128] for j in range(3 if i == 1 else 2)]
+        send([transfer(parts, [(d, T.arr[:, 128 * i:128 * i + 128])], m, S.s0_ if i == 0 else S.s1_)], S.lrel)
+        sent[0] += count(m)
+    if sent[0]:
+        g.wait_ge(S.lrel, sent[0])

@@ -5,38 +5,25 @@ SIM_CORES = 96
 C1, C2 = 0.031, 0.0155
 F8, U8, BF, F32 = "float8_e4m3fn_x4", "uint8", "bfloat16", "float32"
 
-SCRATCH = {
-    "xin": ("sbuf", [128, 512], BF), "w1in": ("sbuf", [128, 1024], BF), "w2in": ("sbuf", [128, 1024], BF),
-    "w34in": ("sbuf", [128, 1536], BF),
-    "xq": ("sbuf", [128, 128], F8), "xs": ("sbuf", [128, 128], U8),
-    "xpq": ("sbuf", [128, 128], F8), "xps": ("sbuf", [128, 128], U8),
-    "xrq": ("sbuf", [128, 256], F8), "xrs": ("sbuf", [128, 256], U8),
-    "w1q": ("sbuf", [128, 256], F8), "w1s": ("sbuf", [128, 256], U8),
-    "w2q": ("sbuf", [128, 256], F8), "w2s": ("sbuf", [128, 256], U8),
-    "woq": ("sbuf", [128, 384], F8), "wos": ("sbuf", [128, 384], U8),
-    "wpq": ("sbuf", [128, 384], F8), "wps": ("sbuf", [128, 384], U8),
-    "w0q": ("sbuf", [128, 384], F8), "w0s": ("sbuf", [128, 384], U8),
-    "w1rq": ("sbuf", [128, 384], F8), "w1rs": ("sbuf", [128, 384], U8),
-    "to": ("sbuf", [128, 512], BF), "tp": ("sbuf", [128, 512], BF), "ta": ("sbuf", [128, 512], BF), "tb": ("sbuf", [128, 512], BF),
-    "tq": ("sbuf", [128, 512], F8), "ts": ("sbuf", [128, 512], U8),
-    "ht": ("sbuf", [128, 512], BF), "hq": ("sbuf", [128, 128], F8), "hs": ("sbuf", [128, 128], U8),
-    "ut": ("sbuf", [128, 2048], BF), "uq": ("sbuf", [128, 512], F8), "us": ("sbuf", [128, 512], U8),
-    "pp": ("sbuf", [128, 256], F32), "pr": ("sbuf", [128, 512], F32),
-    "pd": ("sbuf", [128, 128], F32), "arr": ("sbuf", [128, 256], F32),
-    "a0": ("sbuf", [128, 128], F32), "sm": ("sbuf", [128, 256], F32), "yo": ("sbuf", [128, 128], F32),
-    "rxq": ("sbuf", [128, 256], F8), "rxs": ("sbuf", [128, 256], U8),
-    "rwq": ("sbuf", [128, 384], F8), "rws": ("sbuf", [128, 384], U8),
-    "pin": ("sbuf", [128, 384], F32), "pf": ("sbuf", [128, 128], F32),
-}
+SCRATCH = {}
+for _n, _w in (("xin", 512), ("w1in", 1024), ("w2in", 1024), ("w34in", 1536),
+               ("to", 512), ("tp", 512), ("ta", 512), ("tb", 512), ("ht", 512), ("ut", 2048)):
+    SCRATCH[_n] = ("sbuf", [128, _w], BF)
+for _n, _w in (("x", 128), ("xp", 128), ("xr", 256), ("w1", 256), ("w2", 256), ("wo", 384), ("wp", 384), ("w0f", 384), ("w1f", 384),
+               ("t", 512), ("h", 128), ("u", 512), ("rx", 128), ("rw", 384)):
+    SCRATCH[_n + "q"] = ("sbuf", [128, _w], F8)
+    SCRATCH[_n + "s"] = ("sbuf", [128, _w], U8)
+for _n, _w in (("po", 256), ("pp", 256), ("pr", 512), ("arr", 256), ("yo", 128), ("pf", 256), ("pin", 384)):
+    SCRATCH[_n] = ("sbuf", [128, _w], F32)
 for _b in range(8):
     SCRATCH["b%d" % _b] = ("psum", [128, 512], F32)
 
 SEMAPHORES = (["ld_x", "ld_w1", "ld_w2", "ld_w34", "st"]
-              + ["lx", "lw", "lpp", "lpr", "lrel"]
-              + ["xin_", "xr_", "wp_", "wr0_", "wr1_", "wc_", "ws_", "pd_", "pf_", "pin_", "s0_", "s1_"]
+              + ["lx", "lw", "lpo", "lpp", "lpr", "lrel"]
+              + ["xin_", "xr0_", "xr1_", "wp_", "w0_", "w1_", "wc_", "pf_", "pin_", "s0_", "s1_"]
               + ["q_x", "q_w1", "q_w2", "q_w34", "q_h"]
-              + [a + k for k in "opab" for a in ("z0", "z1", "act", "q_t", "y0", "y1", "act_u", "q_u")]
-              + ["m_po", "m_pp0", "m_pp1", "m_pa0", "m_pa1", "m_pb0", "m_pb1", "cp", "cr", "a0d", "s0d", "s1d", "act_h", "m_y", "y_c"])
+              + [a + k for k in "opab" for a in ("z0", "z1", "act", "q_t", "m0", "m1", "cp", "y0", "y1", "act_u", "q_u")]
+              + ["act_h", "m_y", "y_c"])
 
 
 def plan(T, topo):
@@ -44,34 +31,32 @@ def plan(T, topo):
     chips = sorted({topo.chip(c) for c in cores})
     everyone = range(SIM_CORES)
     on = {ch: [c for c in cores if topo.chip(c) == ch] for ch in chips}
-    far = {c: [d for d in cores if topo.chip(d) != topo.chip(c)] for c in cores}
     mate_of = {c: [d for d in on[topo.chip(c)] if d != c][0] for c in cores}
+    far = {c: sorted([d for d in cores if topo.chip(d) != topo.chip(c)], key=lambda d: topo.die(d) != topo.die(c)) for c in cores}
 
     def owners(ch, die, dst):
-        return [c for c in everyone if c not in cores and topo.chip(c) == ch and topo.die(c) == die and topo.may_write(c, dst)]
-    lane = {}
+        return [c for c in everyone if c not in cores and topo.chip(c) == ch and topo.die(c) == die and topo.may_write(c, dst)][:2]
+    lane, home, wrel = {}, {}, {}
     for d in cores:
-        lane[d] = owners(topo.chip(far[d][0]), topo.die(d), d)[:2]
-    fwd = {}
-    for s in cores:
-        fwd[s] = owners(topo.chip(s), topo.die(s), far[s][0])[1]
-    wrel = {}
-    for s in cores:
-        fc = topo.chip(far[s][0])
-        ch = [m for m in sorted({topo.chip(c) for c in everyone}) if topo.mates(m, fc) and topo.same_plane(m, topo.chip(s))][0]
-        wrel[s] = owners(ch, topo.die(s), far[s][0])[0]
-    return cores, on, far, mate_of, lane, fwd, wrel
+        fc = topo.chip(far[d][0])
+        lane[d] = owners(fc, topo.die(d), d)
+        home[d] = owners(topo.chip(d), topo.die(d), far[d][0])
+        ch = [m for m in sorted({topo.chip(c) for c in everyone}) if topo.mates(m, fc) and topo.same_plane(m, topo.chip(d))][0]
+        wrel[d] = owners(ch, topo.die(d), far[d][0])
+    return cores, on, far, mate_of, lane, home, wrel
+
+
+def u8(ap):
+    return ap.bitcast(dt.uint8)
+
+
+def bits(m):
+    return [1 << i for i in range(m.bit_length()) if (m >> i) & 1]
 
 
 def rank_program(g, core, T, topo):
-    cores, on, far, mate_of, lane, fwd, wrel = plan(T, topo)
+    cores, on, far, mate_of, lane, home, wrel = plan(T, topo)
     S = T.sem
-
-    def u8(ap):
-        return ap.bitcast(dt.uint8)
-
-    def bits(m):
-        return [1 << i for i in range(m.bit_length()) if (m >> i) & 1]
 
     def transfer(srcs, dsts, mask, sem):
         ids = []
@@ -85,205 +70,209 @@ def rank_program(g, core, T, topo):
         g.remote_dma_fused(trs, local_sem=local_sem)
 
     if core not in cores:
-        relay(g, core, T, topo, S, transfer, send, u8)
+        relay(g, core, T, topo, S, transfer, send)
         return
 
-    rank = T.rank_of(core)
     mate = mate_of[core]
     k = on[topo.chip(core)].index(core)
     fa, fb = far[core]
+    ka, kb = [on[topo.chip(f)].index(f) for f in (fa, fb)]
     V, A, P, Y = g.vector, g.scalar, g.tensor, g.sync
 
     Y.dma_start(T.xin[:], T.x[:]).then_inc(S.ld_x, 16)
-    A.dma_start(T.w1in[:], T.w1[:]).then_inc(S.ld_w1, 16)
-    Y.dma_start(T.w34in[:, 0:1024], T.w3[:]).then_inc(S.ld_w34, 16)
     A.dma_start(T.w34in[:, 1024:1536], T.w4[:]).then_inc(S.ld_w34, 16)
+    Y.dma_start(T.w1in[:], T.w1[:]).then_inc(S.ld_w1, 16)
+    A.dma_start(T.w34in[:, 0:1024], T.w3[:]).then_inc(S.ld_w34, 16)
     Y.dma_start(T.w2in[:], T.w2[:]).then_inc(S.ld_w2, 16)
 
     near = topo.mask(core, mate)
     nb = bits(near)
-    off = topo.mask(core, wrel[core])
+    off = topo.mask(core, wrel[core][0])
+    offn = len(bits(off))
     sl = slice(128 * k, 128 * k + 128)
+
+    def halves(buf, o, to, land, sem):
+        return [transfer([buf[:, o + 128 * i:o + 128 * i + 128]], [(to[i], land)], sum(nb[i::2]), sem) for i in (0, 1)]
+
     g.wait_ge(S.q_x, 1)
-    send([transfer([u8(T.xq[:])], [(lane[d][0], u8(T.rxq[:, sl])) for d in (fa, fb)] + [(mate, u8(T.xpq[:]))], near, S.xin_)], S.lx)
-    send([transfer([T.xs[:]], [(lane[d][1], T.rxs[:, sl]) for d in (fa, fb)] + [(mate, T.xps[:])], near, S.xin_)], S.lx)
+    send([transfer([u8(T.xq[:])], [(home[core][0], u8(T.rxq[:]))], near, S.xin_)], S.lx)
+    send([transfer([T.xs[:]], [(home[core][1], T.rxs[:])], near, S.xin_)], S.lx)
+    send([transfer([u8(T.xq[:])], [(mate, u8(T.xpq[:]))], near, S.xin_)], S.lx)
+    send([transfer([T.xs[:]], [(mate, T.xps[:])], near, S.xin_)], S.lx)
     g.wait_ge(S.q_w34, 1)
-    send([transfer([u8(T.woq[:])], [(wrel[core], u8(T.rwq[:]))], off, S.wc_),
+    send([transfer([u8(T.woq[:])], [(wrel[core][0], u8(T.rwq[:]))], off, S.wc_),
           transfer([u8(T.woq[:])], [(mate, u8(T.wpq[:]))], near & ~off, S.wp_)], S.lw)
-    send([transfer([T.wos[:]], [(wrel[core], T.rws[:])], off, S.ws_),
+    send([transfer([T.wos[:]], [(wrel[core][1], T.rws[:])], off, S.wc_),
           transfer([T.wos[:]], [(mate, T.wps[:])], near & ~off, S.wp_)], S.lw)
-    g.wait_ge(S.cp, 2)
-    send([transfer([T.pp[:, 0:128]], [(mate, T.pd[:])], sum(nb[0::2]), S.pd_),
-          transfer([T.pp[:, 128:256]], [(fwd[core], T.pf[:])], sum(nb[1::2]), S.pf_)], S.lpp)
-    g.wait_ge(S.cr, 4)
-    trs = []
-    for i in (0, 1):
-        for n, d in enumerate((fa, fb)):
-            trs.append(transfer([T.pr[:, 256 * n + 128 * i:256 * n + 128 * i + 128]], [(lane[d][i], T.pin[:, sl])],
-                                sum(nb[2 * i + n::4]), S.pin_))
-    send(trs, S.lpr)
-    g.wait_ge(S.lx, 2 * len(nb))
+    g.wait_ge(S.cpo, 2)
+    send(halves(T.po, 0, home[core], T.pf[:, 0:128], S.pf_), S.lpo)
+    g.wait_ge(S.cpp, 2)
+    send(halves(T.pp, 0, home[mate], T.pf[:, 128:256], S.pf_), S.lpp)
+    for n, d in enumerate((fa, fb)):
+        g.wait_ge(S["cp" + "ab"[n]], 2)
+        send(halves(T.pr, 256 * n, lane[d], T.pin[:, sl], S.pin_), S.lpr)
+    g.wait_ge(S.lx, 4 * len(nb))
     g.wait_ge(S.lw, 2 * len(nb))
+    g.wait_ge(S.lpo, len(nb))
     g.wait_ge(S.lpp, len(nb))
-    g.wait_ge(S.lpr, len(nb))
+    g.wait_ge(S.lpr, 2 * len(nb))
 
-    def vact(t, z, b, c, sem, n):
-        V.tensor_scalar(t[0][:, t[1] + b:t[1] + 512:4], z, 0.0, c, AluOpType.max, AluOpType.mult).then_inc(sem, 1)
-        V.tensor_scalar(t[0][:, t[1] + b + 1:t[1] + 512:4], z, 0.0, -c, AluOpType.min, AluOpType.mult).then_inc(sem, 1)
-
-    def sact(t, z, b, c, sem, n):
-        A.activation(t[0][:, t[1] + b:t[1] + 512:4], z, ActivationFunctionType.Relu, scale=c).then_inc(sem, 1)
-        A.activation(t[0][:, t[1] + b + 1:t[1] + 512:4], z, ActivationFunctionType.Relu, scale=-c).then_inc(sem, 1)
-
-    tiles = {"o": (T.to, 0), "p": (T.tp, 0), "a": (T.ta, 0), "b": (T.tb, 0)}
-    col = {"o": 0, "p": 128, "a": 256, "b": 384}
+    tiles = {"o": T.to, "p": T.tp, "a": T.ta, "b": T.tb}
+    idx = {"o": 0, "p": 1, "a": 2, "b": 3}
     zb = {"o": (T.b0, T.b1), "p": (T.b4, T.b5), "a": (T.b0, T.b1), "b": (T.b4, T.b5)}
     pb = {"o": (T.b2, T.b3), "p": (T.b6, T.b7), "a": (T.b0, T.b1), "b": (T.b4, T.b5)}
-    ub = {"o": (T.b6, T.b7), "p": (T.b0, T.b1), "a": (T.b4, T.b5), "b": (T.b2, T.b3)}
-    xin = {"o": (T.xq[:], T.xs[:]), "p": (T.xpq[:], T.xps[:]),
-           "a": (T.xrq[:, 0:128], T.xrs[:, 0:128]), "b": (T.xrq[:, 128:256], T.xrs[:, 128:256])}
-    wg = {"o": (T.woq, T.wos), "p": (T.wpq, T.wps), "a": (T.w0q, T.w0s), "b": (T.w1rq, T.w1rs)}
+    ub = {"o": (T.b6, T.b7), "p": (T.b2, T.b3), "a": (T.b0, T.b1), "b": (T.b4, T.b5)}
+    pbuf = {"o": (T.po, 0), "p": (T.pp, 0), "a": (T.pr, 0), "b": (T.pr, 256)}
+    W1, W2, TC, UC, XR = (T.w1q, T.w1s), (T.w2q, T.w2s), (T.tq, T.ts), (T.uq, T.us), (T.xrq, T.xrs)
+    wf = ((T.w0fq, T.w0fs), (T.w1fq, T.w1fs))
+    wg = {"o": (T.woq, T.wos), "p": (T.wpq, T.wps), "a": wf[ka], "b": wf[kb]}
 
-    def w_t(q, s, i):
-        return q[:, 128 * i:128 * i + 128], s[:, 128 * i:128 * i + 128]
+    def part(w, i):
+        return w[0][:, 128 * i:128 * i + 128], w[1][:, 128 * i:128 * i + 128]
+    xin = {"o": (T.xq[:], T.xs[:]), "p": (T.xpq[:], T.xps[:]), "a": part(XR, ka), "b": part(XR, kb)}
 
     def mm(out, w, x, sem, start=True, stop=True):
         ins = P.matmul_mx(out[:, 0:128], w[0], w[1], x[0], x[1], start, stop)
         if sem is not None:
             ins.then_inc(sem, 1)
 
-    def tcodes(c):
-        return T.tq[:, col[c]:col[c] + 128], T.ts[:, col[c]:col[c] + 128]
+    def sign(e, t, o, z, b, c, sem):
+        out = t[:, o + b:o + 512:4]
+        if e == "A":
+            ins = A.activation(out, z, ActivationFunctionType.Relu, scale=c if b % 2 == 0 else -c)
+        elif b % 2 == 0:
+            ins = V.tensor_scalar(out, z, 0.0, c, AluOpType.max, AluOpType.mult)
+        else:
+            ins = V.tensor_scalar(out, z, 0.0, -c, AluOpType.min, AluOpType.mult)
+        ins.then_inc(sem, 1)
 
-    def ucodes(c):
-        return T.uq[:, col[c]:col[c] + 128], T.us[:, col[c]:col[c] + 128]
+    def quant(q, s, src, sem):
+        V.quantize_mx(q, s, src).then_inc(sem, 1)
+
+    def on_q(e):
+        return V if e == "V" else A
+
+    def tz(e, c, i):
+        on_q(e).wait_ge(S["z%d%s" % (i, c)], 1)
+        for b in (0, 1):
+            sign(e, tiles[c], 0, zb[c][i][:, 0:128], 2 * i + b, C1, S["act" + c])
+
+    def tq(c):
+        V.wait_ge(S["act" + c], 4)
+        q, s = part(TC, idx[c])
+        quant(q, s, tiles[c][:], S["q_t" + c])
+
+    def pcopy(e, c, i):
+        on_q(e).wait_ge(S["m%d%s" % (i, c)], 1)
+        buf, o = pbuf[c]
+        out, z = buf[:, o + 128 * i:o + 128 * i + 128], pb[c][i][:, 0:128]
+        ins = V.tensor_copy(out, z) if e == "V" else A.activation(out, z, ActivationFunctionType.Copy)
+        ins.then_inc(S["cp" + c], 1)
+
+    def uz(e, c, i):
+        on_q(e).wait_ge(S["y%d%s" % (i, c)], 1)
+        for b in (0, 1):
+            sign(e, T.ut, 512 * idx[c], ub[c][i][:, 0:128], 2 * i + b, C1, S["act_u" + c])
+
+    def uq(c):
+        V.wait_ge(S["act_u" + c], 4)
+        q, s = part(UC, idx[c])
+        quant(q, s, T.ut[:, 512 * idx[c]:512 * idx[c] + 512], S["q_u" + c])
+
+    def tensor_z(c):
+        for i in (0, 1):
+            mm(zb[c][i], part(W1, i), xin[c], S["z%d%s" % (i, c)])
+
+    def tensor_p(c):
+        P.wait_ge(S["q_t" + c], 1)
+        for i in (0, 1):
+            mm(pb[c][i], part(W2, i), part(TC, idx[c]), S["m%d%s" % (i, c)])
 
     P.wait_ge(S.q_x, 1)
     P.wait_ge(S.q_w1, 1)
-    for i in (0, 1):
-        mm(zb["o"][i], w_t(T.w1q, T.w1s, i), xin["o"], S["z%do" % i])
+    tensor_z("o")
     P.wait_ge(S.q_w2, 1)
-    P.wait_ge(S.q_to, 1)
-    for i in (0, 1):
-        mm(pb["o"][i], w_t(T.w2q, T.w2s, i), tcodes("o"), S.m_po)
+    tensor_p("o")
     P.wait_ge(S.xin_, 2 * len(nb))
-    for i in (0, 1):
-        mm(zb["p"][i], w_t(T.w1q, T.w1s, i), xin["p"], S["z%dp" % i])
-    P.wait_ge(S.q_tp, 1)
-    for i in (0, 1):
-        mm(pb["p"][i], w_t(T.w2q, T.w2s, i), tcodes("p"), S["m_pp%d" % i])
-    offn = len(bits(off))
-    P.wait_ge(S.xr_, 2 * offn)
-    for c in "ab":
-        for i in (0, 1):
-            mm(zb[c][i], w_t(T.w1q, T.w1s, i), xin[c], S["z%d%s" % (i, c)])
-    for c in "ab":
-        P.wait_ge(S["q_t" + c], 1)
-        for i in (0, 1):
-            mm(pb[c][i], w_t(T.w2q, T.w2s, i), tcodes(c), S["m_p%s%d" % (c, i)])
-    P.wait_ge(S.cp, 2)
-    P.wait_ge(S.cr, 4)
+    tensor_z("p")
+    tensor_p("p")
+    P.wait_ge(S["xr%d_" % ka], 2 * offn)
+    tensor_z("a")
+    P.wait_ge(S["xr%d_" % kb], 2 * offn)
+    tensor_z("b")
+    tensor_p("a")
+    tensor_p("b")
+    for c in "opab":
+        P.wait_ge(S["cp" + c], 2)
     P.wait_ge(S.q_h, 1)
     for c in "opab":
         if c == "p":
             P.wait_ge(S.wp_, 2 * (len(nb) - offn))
         if c in "ab":
-            P.wait_ge(S["wr%d_" % "ab".index(c)], 2 * offn)
-        for i in (0, 1):
-            mm(ub[c][i], w_t(wg[c][0], wg[c][1], i), (T.hq[:], T.hs[:]), S["y%d%s" % (i, c)])
+            P.wait_ge(S["w%d_" % (ka if c == "a" else kb)], 2 * offn)
+        for i in ((0, 1) if c == "b" else (1, 0)):
+            mm(ub[c][i], part(wg[c], i), (T.hq[:], T.hs[:]), S["y%d%s" % (i, c)])
     for c in "opab":
         P.wait_ge(S["q_u" + c], 1)
-        mm(T.b6, w_t(wg[c][0], wg[c][1], 2), ucodes(c), S.m_y if c == "b" else None, c == "o", c == "b")
-
-    def quant(dst, src, sem):
-        V.quantize_mx(dst[0], dst[1], src).then_inc(sem, 1)
-
-    def vtile(c):
-        V.wait_ge(S["z0" + c], 1)
-        vact(tiles[c], zb[c][0][:, 0:128], 0, C1, S["act" + c], 2)
-
-    def vquant(c):
-        V.wait_ge(S["act" + c], 4)
-        quant(tcodes(c), tiles[c][0][:], S["q_t" + c])
+        mm(T.b6, part(wg[c], 2), part(UC, idx[c]), S.m_y if c == "b" else None, c == "o", c == "b")
 
     V.wait_ge(S.ld_x, 16)
-    quant((T.xq[:], T.xs[:]), T.xin[:], S.q_x)
+    quant(T.xq[:], T.xs[:], T.xin[:], S.q_x)
     V.wait_ge(S.ld_w1, 16)
-    quant((T.w1q[:], T.w1s[:]), T.w1in[:], S.q_w1)
+    quant(T.w1q[:], T.w1s[:], T.w1in[:], S.q_w1)
     V.wait_ge(S.ld_w34, 32)
-    quant((T.woq[:], T.wos[:]), T.w34in[:], S.q_w34)
-    vtile("o")
-    vquant("o")
+    quant(T.woq[:], T.wos[:], T.w34in[:], S.q_w34)
+    tz("V", "o", 0)
+    tq("o")
     V.wait_ge(S.ld_w2, 16)
-    quant((T.w2q[:], T.w2s[:]), T.w2in[:], S.q_w2)
-    vtile("p")
-    vquant("p")
-    V.wait_ge(S.m_pp0, 1)
-    V.tensor_copy(T.pp[:, 0:128], pb["p"][0][:, 0:128]).then_inc(S.cp, 1)
-    vtile("a")
-    vtile("b")
-    vquant("a")
-    vquant("b")
+    quant(T.w2q[:], T.w2s[:], T.w2in[:], S.q_w2)
+    pcopy("V", "o", 0)
+    tz("V", "p", 0)
+    tq("p")
+    pcopy("V", "p", 0)
+    tz("V", "a", 0)
+    tq("a")
+    tz("V", "b", 0)
+    tq("b")
+    pcopy("V", "b", 0)
     for i in (0, 1):
-        V.wait_ge(S["m_pb%d" % i], 1)
-        V.tensor_copy(T.pr[:, 256 + 128 * i:384 + 128 * i], pb["b"][i][:, 0:128]).then_inc(S.cr, 1)
-    V.wait_ge(S.m_po, 2)
-    V.wait_ge(S.pd_, len(nb) // 2)
-    V.tensor_tensor(T.a0[:], pb["o"][0][:, 0:128], T.pd[:], AluOpType.add).then_inc(S.a0d, 1)
-    V.wait_ge(S.a0d, 1)
-    V.wait_ge(S.s0_, offn)
-    V.tensor_tensor(T.sm[:, 0:128], T.a0[:], T.arr[:, 0:128], AluOpType.add).then_inc(S.s0d, 1)
-    V.wait_ge(S.s1_, offn)
-    V.tensor_tensor(T.sm[:, 128:256], pb["o"][1][:, 0:128], T.arr[:, 128:256], AluOpType.add).then_inc(S.s1d, 1)
-    V.wait_ge(S.s0d, 1)
-    vact((T.ht, 0), T.sm[:, 0:128], 0, C2, S.act_h, 2)
+        V.wait_ge(S["s%d_" % i], offn)
+        sign("V", T.ht, 0, T.arr[:, 128 * i:128 * i + 128], 2 * i, C2, S.act_h)
     V.wait_ge(S.act_h, 4)
-    quant((T.hq[:], T.hs[:]), T.ht[:], S.q_h)
-
-    def vu(c):
-        V.wait_ge(S["y0" + c], 1)
-        vact((T.ut, 4 * col[c]), ub[c][0][:, 0:128], 0, C1, S["act_u" + c], 2)
-
-    def vuq(c):
-        V.wait_ge(S["act_u" + c], 4)
-        quant(ucodes(c), T.ut[:, 4 * col[c]:4 * col[c] + 512], S["q_u" + c])
-    vu("o")
-    vu("p")
-    vuq("o")
-    vu("a")
-    vuq("p")
-    vu("b")
-    vuq("a")
-    vuq("b")
+    quant(T.hq[:], T.hs[:], T.ht[:], S.q_h)
+    uz("V", "o", 0)
+    uq("o")
+    uz("V", "p", 0)
+    uq("p")
+    uz("V", "b", 0)
+    uq("a")
+    uq("b")
     V.wait_ge(S.m_y, 1)
     V.tensor_copy(T.yo[:], T.b6[:, 0:128]).then_inc(S.y_c, 1)
 
-    def stile(c):
-        A.wait_ge(S["z1" + c], 1)
-        sact(tiles[c], zb[c][1][:, 0:128], 2, C1, S["act" + c], 2)
-    stile("o")
-    stile("p")
-    A.wait_ge(S.m_pp1, 1)
-    A.activation(T.pp[:, 128:256], pb["p"][1][:, 0:128], ActivationFunctionType.Copy).then_inc(S.cp, 1)
-    stile("a")
-    stile("b")
+    tz("A", "o", 1)
+    pcopy("A", "o", 1)
+    tz("A", "p", 1)
+    pcopy("A", "p", 1)
+    tz("A", "a", 1)
+    tz("A", "b", 1)
+    pcopy("A", "a", 0)
+    pcopy("A", "a", 1)
+    pcopy("A", "b", 1)
     for i in (0, 1):
-        A.wait_ge(S["m_pa%d" % i], 1)
-        A.activation(T.pr[:, 128 * i:128 * i + 128], pb["a"][i][:, 0:128], ActivationFunctionType.Copy).then_inc(S.cr, 1)
-    A.wait_ge(S.s1d, 1)
-    sact((T.ht, 0), T.sm[:, 128:256], 2, C2, S.act_h, 2)
-    for c in "opab":
-        A.wait_ge(S["y1" + c], 1)
-        sact((T.ut, 4 * col[c]), ub[c][1][:, 0:128], 2, C1, S["act_u" + c], 2)
+        A.wait_ge(S["s%d_" % i], offn)
+        sign("A", T.ht, 0, T.arr[:, 128 * i:128 * i + 128], 2 * i + 1, C2, S.act_h)
+    for c, i in (("o", 1), ("p", 1), ("a", 1), ("a", 0), ("b", 1)):
+        uz("A", c, i)
 
     Y.wait_ge(S.lw, 2 * len(nb))
     for c, d in (("o", core), ("p", mate)):
         Y.wait_ge(S["act" + c], 4)
-        Y.dma_start(T.t[T.rank_of(d)], tiles[c][0][:]).then_inc(S.st, 16)
-    Y.wait_ge(S.lpr, len(nb))
+        Y.dma_start(T.t[T.rank_of(d)], tiles[c][:]).then_inc(S.st, 16)
+    Y.wait_ge(S.lpr, 2 * len(nb))
     for c, d in (("a", fa), ("b", fb)):
         Y.wait_ge(S["act" + c], 4)
-        Y.dma_start(T.t[T.rank_of(d)], tiles[c][0][:]).then_inc(S.st, 16)
+        Y.dma_start(T.t[T.rank_of(d)], tiles[c][:]).then_inc(S.st, 16)
     Y.wait_ge(S.act_h, 4)
     Y.dma_start(T.h[:], T.ht[:]).then_inc(S.st, 16)
     Y.wait_ge(S.y_c, 1)
@@ -291,51 +280,44 @@ def rank_program(g, core, T, topo):
     Y.wait_ge(S.st, 96)
 
 
-def relay(g, core, T, topo, S, transfer, send, u8):
-    cores, on, far, mate_of, lane, fwd, wrel = plan(T, topo)
+def relay(g, core, T, topo, S, transfer, send):
+    cores, on, far, mate_of, lane, home, wrel = plan(T, topo)
     sent = [0]
 
     def count(m):
-        return sum((m >> i) & 1 for i in range(m.bit_length()))
+        return len(bits(m))
+
+    def out(srcs, dsts, sem):
+        m = topo.mask(core, dsts[0][0])
+        send([transfer(srcs, dsts, m, sem)], S.lrel)
+        sent[0] += count(m)
 
     for s in cores:
-        if wrel[s] == core:
+        if core in wrel[s]:
             k = on[topo.chip(s)].index(s)
-            m = topo.mask(core, far[s][0])
-            n = count(topo.mask(s, core))
-            q, p, sem = (T.w0q, T.w0s, S.wr0_) if k == 0 else (T.w1rq, T.w1rs, S.wr1_)
-            g.wait_ge(S.wc_, n)
-            send([transfer([u8(T.rwq[:])], [(d, u8(q[:])) for d in far[s]], m, sem)], S.lrel)
-            g.wait_ge(S.ws_, n)
-            send([transfer([T.rws[:]], [(d, p[:]) for d in far[s]], m, sem)], S.lrel)
-            sent[0] += 2 * count(m)
+            g.wait_ge(S.wc_, count(topo.mask(s, core)))
+            if core == wrel[s][0]:
+                out([u8(T.rwq[:])], [(d, u8(T["w%dfq" % k][:])) for d in far[s]], S["w%d_" % k])
+            else:
+                out([T.rws[:]], [(d, T["w%dfs" % k][:]) for d in far[s]], S["w%d_" % k])
     for d in cores:
-        if core not in lane[d]:
-            continue
-        i = lane[d].index(core)
-        srcs = far[d]
-        m = topo.mask(core, d)
-        near = count(topo.mask(srcs[0], core))
-        g.wait_ge(S.xin_, 2 * near)
-        if i == 0:
-            send([transfer([u8(T.rxq[:])], [(d, u8(T.xrq[:]))], m, S.xr_)], S.lrel)
-        else:
-            send([transfer([T.rxs[:]], [(d, T.xrs[:])], m, S.xr_)], S.lrel)
-        sent[0] += count(m)
-        extra = 0
-        for s in srcs:
-            if fwd[s] == core:
-                to = lane[mate_of[s]][1]
-                g.wait_ge(S.pf_, near // 2)
-                mm = topo.mask(core, to)
-                send([transfer([T.pf[:]], [(to, T.pin[:, 256:384])], mm, S.pin_)], S.lrel)
-                sent[0] += count(mm)
-        if i == 1:
-            s = mate_of[d]
-            extra = count(topo.mask(fwd[s], core))
-        g.wait_ge(S.pin_, near // 2 + extra)
-        parts = [T.pin[:, 128 * j:128 * j + 128] for j in range(3 if i == 1 else 2)]
-        send([transfer(parts, [(d, T.arr[:, 128 * i:128 * i + 128])], m, S.s0_ if i == 0 else S.s1_)], S.lrel)
-        sent[0] += count(m)
+        if core in home[d]:
+            k = on[topo.chip(d)].index(d)
+            cols = slice(128 * k, 128 * k + 128)
+            g.wait_ge(S.xin_, count(topo.mask(d, core)))
+            if core == home[d][0]:
+                out([u8(T.rxq[:])], [(f, u8(T.xrq[:, cols])) for f in far[d]], S["xr%d_" % k])
+            else:
+                out([T.rxs[:]], [(f, T.xrs[:, cols]) for f in far[d]], S["xr%d_" % k])
+    for d in cores:
+        if core in home[d]:
+            i = home[d].index(core)
+            g.wait_ge(S.pf_, count(topo.mask(d, core)))
+            out([T.pf[:, 0:128], T.pf[:, 128:256]], [(lane[d][i], T.pin[:, 256:384])], S.pin_)
+    for d in cores:
+        if core in lane[d]:
+            i = lane[d].index(core)
+            g.wait_ge(S.pin_, count(topo.mask(far[d][0], core)) + count(topo.mask(home[d][i], core)))
+            out([T.pin[:, 128 * j:128 * j + 128] for j in range(3)], [(d, T.arr[:, 128 * i:128 * i + 128])], S["s%d_" % i])
     if sent[0]:
         g.wait_ge(S.lrel, sent[0])

from concourse.bass import DstId, RemoteDMATransfer
from concourse.mybir import dt, AluOpType, ActivationFunctionType

SIM_CORES = 96
C1, C2 = 0.031, 0.0155
F8, U8, BF, F32 = "float8_e4m3fn_x4", "uint8", "bfloat16", "float32"

SCRATCH = {}
for _n, _w in (("xin", 512), ("w1in", 1024), ("w2in", 1024), ("w34in", 1536),
               ("to", 512), ("tp", 512), ("ta", 512), ("tb", 512), ("ht", 512), ("ut", 2048)):
    SCRATCH[_n] = ("sbuf", [128, _w], BF)
for _n, _w in (("x", 128), ("xp", 128), ("xr", 256), ("w1", 256), ("w2", 256), ("wo", 384), ("wp", 384), ("w0f", 384), ("w1f", 384),
               ("t", 512), ("h", 128), ("u", 512), ("rx", 128), ("rw", 384)):
    SCRATCH[_n + "q"] = ("sbuf", [128, _w], F8)
    SCRATCH[_n + "s"] = ("sbuf", [128, _w], U8)
for _n, _w in (("po", 256), ("pp", 256), ("pr", 512), ("arr", 256), ("yo", 128), ("pf", 256), ("pin", 384)):
    SCRATCH[_n] = ("sbuf", [128, _w], F32)
for _b in range(8):
    SCRATCH["b%d" % _b] = ("psum", [128, 512], F32)

SEMAPHORES = (["ld_x", "ld_w1", "ld_w2", "ld_w34", "st"]
              + ["lx", "lw", "lpo", "lpp", "lpr", "lrel"]
              + ["xin_", "xr0_", "xr1_", "wp_", "w0_", "w1_", "wc_", "pf_", "pin_", "s0_", "s1_"]
              + ["q_x", "q_w1", "q_w2", "q_w34", "q_h"]
              + [a + k for k in "opab" for a in ("z0", "z1", "act", "q_t", "m0", "m1", "cp", "y0", "y1", "act_u", "q_u")]
              + ["act_h", "m_y", "y_c"])


def plan(T, topo):
    cores = list(T.cores)
    chips = sorted({topo.chip(c) for c in cores})
    everyone = range(SIM_CORES)
    on = {ch: [c for c in cores if topo.chip(c) == ch] for ch in chips}
    mate_of = {c: [d for d in on[topo.chip(c)] if d != c][0] for c in cores}
    far = {c: sorted([d for d in cores if topo.chip(d) != topo.chip(c)], key=lambda d: topo.die(d) != topo.die(c)) for c in cores}

    def owners(ch, die, dst):
        return [c for c in everyone if c not in cores and topo.chip(c) == ch and topo.die(c) == die and topo.may_write(c, dst)][:2]
    lane, home, wrel = {}, {}, {}
    for d in cores:
        fc = topo.chip(far[d][0])
        lane[d] = owners(fc, topo.die(d), d)
        home[d] = owners(topo.chip(d), topo.die(d), far[d][0])
        ch = [m for m in sorted({topo.chip(c) for c in everyone}) if topo.mates(m, fc) and topo.same_plane(m, topo.chip(d))][0]
        wrel[d] = owners(ch, topo.die(d), far[d][0])
    return cores, on, far, mate_of, lane, home, wrel


def u8(ap):
    return ap.bitcast(dt.uint8)


def bits(m):
    return [1 << i for i in range(m.bit_length()) if (m >> i) & 1]


def rank_program(g, core, T, topo):
    cores, on, far, mate_of, lane, home, wrel = plan(T, topo)
    S = T.sem

    def transfer(srcs, dsts, mask, sem):
        ids = []
        for c, _ in dsts:
            rid, pid, _se = topo.addr(c)
            ids.append(DstId(rid=rid, pnc=pid))
        return RemoteDMATransfer(dst_ids=ids, srcs=srcs, dsts=[ap for _, ap in dsts], dma_engine_mask=mask,
                                 remote_sem=sem, alu_op=1 if len(srcs) > 1 else 0)

    def send(trs, local_sem):
        g.remote_dma_fused(trs, local_sem=local_sem)

    if core not in cores:
        relay(g, core, T, topo, S, transfer, send)
        return

    mate = mate_of[core]
    k = on[topo.chip(core)].index(core)
    fa, fb = far[core]
    ka, kb = [on[topo.chip(f)].index(f) for f in (fa, fb)]
    V, A, P, Y = g.vector, g.scalar, g.tensor, g.sync

    Y.dma_start(T.xin[:], T.x[:]).then_inc(S.ld_x, 16)
    A.dma_start(T.w34in[:, 1024:1536], T.w4[:]).then_inc(S.ld_w34, 16)
    Y.dma_start(T.w1in[:], T.w1[:]).then_inc(S.ld_w1, 16)
    A.dma_start(T.w34in[:, 0:1024], T.w3[:]).then_inc(S.ld_w34, 16)
    Y.dma_start(T.w2in[:], T.w2[:]).then_inc(S.ld_w2, 16)

    near = topo.mask(core, mate)
    nb = bits(near)
    off = topo.mask(core, wrel[core][0])
    offn = len(bits(off))
    sl = slice(128 * k, 128 * k + 128)

    def halves(buf, o, to, land, sem):
        return [transfer([buf[:, o + 128 * i:o + 128 * i + 128]], [(to[i], land)], sum(nb[i::2]), sem) for i in (0, 1)]

    g.wait_ge(S.q_x, 1)
    send([transfer([u8(T.xq[:])], [(home[core][0], u8(T.rxq[:]))], near, S.xin_)], S.lx)
    send([transfer([T.xs[:]], [(home[core][1], T.rxs[:])], near, S.xin_)], S.lx)
    send([transfer([u8(T.xq[:])], [(mate, u8(T.xpq[:]))], near, S.xin_)], S.lx)
    send([transfer([T.xs[:]], [(mate, T.xps[:])], near, S.xin_)], S.lx)
    g.wait_ge(S.q_w34, 1)
    send([transfer([u8(T.woq[:])], [(wrel[core][0], u8(T.rwq[:]))], off, S.wc_),
          transfer([u8(T.woq[:])], [(mate, u8(T.wpq[:]))], near & ~off, S.wp_)], S.lw)
    send([transfer([T.wos[:]], [(wrel[core][1], T.rws[:])], off, S.wc_),
          transfer([T.wos[:]], [(mate, T.wps[:])], near & ~off, S.wp_)], S.lw)
    g.wait_ge(S.cpo, 2)
    send(halves(T.po, 0, home[core], T.pf[:, 0:128], S.pf_), S.lpo)
    g.wait_ge(S.cpp, 2)
    send(halves(T.pp, 0, home[mate], T.pf[:, 128:256], S.pf_), S.lpp)
    for n, d in enumerate((fa, fb)):
        g.wait_ge(S["cp" + "ab"[n]], 2)
        send(halves(T.pr, 256 * n, lane[d], T.pin[:, sl], S.pin_), S.lpr)
    g.wait_ge(S.lx, 4 * len(nb))
    g.wait_ge(S.lw, 2 * len(nb))
    g.wait_ge(S.lpo, len(nb))
    g.wait_ge(S.lpp, len(nb))
    g.wait_ge(S.lpr, 2 * len(nb))

    tiles = {"o": T.to, "p": T.tp, "a": T.ta, "b": T.tb}
    idx = {"o": 0, "p": 1, "a": 2, "b": 3}
    zb = {"o": (T.b0, T.b1), "p": (T.b4, T.b5), "a": (T.b0, T.b1), "b": (T.b4, T.b5)}
    pb = {"o": (T.b2, T.b3), "p": (T.b6, T.b7), "a": (T.b0, T.b1), "b": (T.b4, T.b5)}
    ub = {"o": (T.b6, T.b7), "p": (T.b2, T.b3), "a": (T.b0, T.b1), "b": (T.b4, T.b5)}
    pbuf = {"o": (T.po, 0), "p": (T.pp, 0), "a": (T.pr, 0), "b": (T.pr, 256)}
    W1, W2, TC, UC, XR = (T.w1q, T.w1s), (T.w2q, T.w2s), (T.tq, T.ts), (T.uq, T.us), (T.xrq, T.xrs)
    wf = ((T.w0fq, T.w0fs), (T.w1fq, T.w1fs))
    wg = {"o": (T.woq, T.wos), "p": (T.wpq, T.wps), "a": wf[ka], "b": wf[kb]}

    def part(w, i):
        return w[0][:, 128 * i:128 * i + 128], w[1][:, 128 * i:128 * i + 128]
    xin = {"o": (T.xq[:], T.xs[:]), "p": (T.xpq[:], T.xps[:]), "a": part(XR, ka), "b": part(XR, kb)}

    def mm(out, w, x, sem, start=True, stop=True):
        ins = P.matmul_mx(out[:, 0:128], w[0], w[1], x[0], x[1], start, stop)
        if sem is not None:
            ins.then_inc(sem, 1)

    def sign(e, t, o, z, b, c, sem):
        out = t[:, o + b:o + 512:4]
        if e == "A":
            ins = A.activation(out, z, ActivationFunctionType.Relu, scale=c if b % 2 == 0 else -c)
        elif b % 2 == 0:
            ins = V.tensor_scalar(out, z, 0.0, c, AluOpType.max, AluOpType.mult)
        else:
            ins = V.tensor_scalar(out, z, 0.0, -c, AluOpType.min, AluOpType.mult)
        ins.then_inc(sem, 1)

    def quant(q, s, src, sem):
        V.quantize_mx(q, s, src).then_inc(sem, 1)

    def on_q(e):
        return V if e == "V" else A

    def tz(e, c, i):
        on_q(e).wait_ge(S["z%d%s" % (i, c)], 1)
        for b in (0, 1):
            sign(e, tiles[c], 0, zb[c][i][:, 0:128], 2 * i + b, C1, S["act" + c])

    def tq(c):
        V.wait_ge(S["act" + c], 4)
        q, s = part(TC, idx[c])
        quant(q, s, tiles[c][:], S["q_t" + c])

    def pcopy(e, c, i):
        on_q(e).wait_ge(S["m%d%s" % (i, c)], 1)
        buf, o = pbuf[c]
        out, z = buf[:, o + 128 * i:o + 128 * i + 128], pb[c][i][:, 0:128]
        ins = V.tensor_copy(out, z) if e == "V" else A.activation(out, z, ActivationFunctionType.Copy)
        ins.then_inc(S["cp" + c], 1)

    def uz(e, c, i):
        on_q(e).wait_ge(S["y%d%s" % (i, c)], 1)
        for b in (0, 1):
            sign(e, T.ut, 512 * idx[c], ub[c][i][:, 0:128], 2 * i + b, C1, S["act_u" + c])

    def uq(c):
        V.wait_ge(S["act_u" + c], 4)
        q, s = part(UC, idx[c])
        quant(q, s, T.ut[:, 512 * idx[c]:512 * idx[c] + 512], S["q_u" + c])

    def tensor_z(c):
        for i in (0, 1):
            mm(zb[c][i], part(W1, i), xin[c], S["z%d%s" % (i, c)])

    def tensor_p(c):
        P.wait_ge(S["q_t" + c], 1)
        for i in (0, 1):
            mm(pb[c][i], part(W2, i), part(TC, idx[c]), S["m%d%s" % (i, c)])

    P.wait_ge(S.q_x, 1)
    P.wait_ge(S.q_w1, 1)
    tensor_z("o")
    P.wait_ge(S.q_w2, 1)
    tensor_p("o")
    P.wait_ge(S.xin_, 2 * len(nb))
    tensor_z("p")
    tensor_p("p")
    P.wait_ge(S["xr%d_" % ka], 2 * offn)
    tensor_z("a")
    P.wait_ge(S["xr%d_" % kb], 2 * offn)
    tensor_z("b")
    tensor_p("a")
    tensor_p("b")
    for c in "opab":
        P.wait_ge(S["cp" + c], 2)
    P.wait_ge(S.q_h, 1)
    for c in "opab":
        if c == "p":
            P.wait_ge(S.wp_, 2 * (len(nb) - offn))
        if c in "ab":
            P.wait_ge(S["w%d_" % (ka if c == "a" else kb)], 2 * offn)
        for i in ((0, 1) if c == "b" else (1, 0)):
            mm(ub[c][i], part(wg[c], i), (T.hq[:], T.hs[:]), S["y%d%s" % (i, c)])
    for c in "opab":
        P.wait_ge(S["q_u" + c], 1)
        mm(T.b6, part(wg[c], 2), part(UC, idx[c]), S.m_y if c == "b" else None, c == "o", c == "b")

    V.wait_ge(S.ld_x, 16)
    quant(T.xq[:], T.xs[:], T.xin[:], S.q_x)
    V.wait_ge(S.ld_w1, 16)
    quant(T.w1q[:], T.w1s[:], T.w1in[:], S.q_w1)
    V.wait_ge(S.ld_w34, 32)
    quant(T.woq[:], T.wos[:], T.w34in[:], S.q_w34)
    tz("V", "o", 0)
    tq("o")
    V.wait_ge(S.ld_w2, 16)
    quant(T.w2q[:], T.w2s[:], T.w2in[:], S.q_w2)
    pcopy("V", "o", 0)
    tz("V", "p", 0)
    tq("p")
    pcopy("V", "p", 0)
    tz("V", "a", 0)
    tq("a")
    tz("V", "b", 0)
    tq("b")
    pcopy("V", "b", 0)
    for i in (0, 1):
        V.wait_ge(S["s%d_" % i], offn)
        sign("V", T.ht, 0, T.arr[:, 128 * i:128 * i + 128], 2 * i, C2, S.act_h)
    V.wait_ge(S.act_h, 4)
    quant(T.hq[:], T.hs[:], T.ht[:], S.q_h)
    uz("V", "o", 0)
    uq("o")
    uz("V", "p", 0)
    uq("p")
    uz("V", "b", 0)
    uq("a")
    uq("b")
    V.wait_ge(S.m_y, 1)
    V.tensor_copy(T.yo[:], T.b6[:, 0:128]).then_inc(S.y_c, 1)

    tz("A", "o", 1)
    pcopy("A", "o", 1)
    tz("A", "p", 1)
    pcopy("A", "p", 1)
    tz("A", "a", 1)
    tz("A", "b", 1)
    pcopy("A", "a", 0)
    pcopy("A", "a", 1)
    pcopy("A", "b", 1)
    for i in (0, 1):
        A.wait_ge(S["s%d_" % i], offn)
        sign("A", T.ht, 0, T.arr[:, 128 * i:128 * i + 128], 2 * i + 1, C2, S.act_h)
    for c, i in (("o", 1), ("p", 1), ("a", 1), ("a", 0), ("b", 1)):
        uz("A", c, i)

    Y.wait_ge(S.lw, 2 * len(nb))
    for c, d in (("o", core), ("p", mate)):
        Y.wait_ge(S["act" + c], 4)
        Y.dma_start(T.t[T.rank_of(d)], tiles[c][:]).then_inc(S.st, 16)
    Y.wait_ge(S.lpr, 2 * len(nb))
    for c, d in (("a", fa), ("b", fb)):
        Y.wait_ge(S["act" + c], 4)
        Y.dma_start(T.t[T.rank_of(d)], tiles[c][:]).then_inc(S.st, 16)
    Y.wait_ge(S.act_h, 4)
    Y.dma_start(T.h[:], T.ht[:]).then_inc(S.st, 16)
    Y.wait_ge(S.y_c, 1)
    Y.dma_start(T.y[:], T.yo[:]).then_inc(S.st, 16)
    Y.wait_ge(S.st, 96)


def relay(g, core, T, topo, S, transfer, send):
    cores, on, far, mate_of, lane, home, wrel = plan(T, topo)
    sent = [0]

    def count(m):
        return len(bits(m))

    def out(srcs, dsts, sem):
        m = topo.mask(core, dsts[0][0])
        send([transfer(srcs, dsts, m, sem)], S.lrel)
        sent[0] += count(m)

    for s in cores:
        if core in wrel[s]:
            k = on[topo.chip(s)].index(s)
            g.wait_ge(S.wc_, count(topo.mask(s, core)))
            if core == wrel[s][0]:
                out([u8(T.rwq[:])], [(d, u8(T["w%dfq" % k][:])) for d in far[s]], S["w%d_" % k])
            else:
                out([T.rws[:]], [(d, T["w%dfs" % k][:]) for d in far[s]], S["w%d_" % k])
    for d in cores:
        if core in home[d]:
            k = on[topo.chip(d)].index(d)
            cols = slice(128 * k, 128 * k + 128)
            g.wait_ge(S.xin_, count(topo.mask(d, core)))
            if core == home[d][0]:
                out([u8(T.rxq[:])], [(f, u8(T.xrq[:, cols])) for f in far[d]], S["xr%d_" % k])
            else:
                out([T.rxs[:]], [(f, T.xrs[:, cols]) for f in far[d]], S["xr%d_" % k])
    for d in cores:
        if core in home[d]:
            i = home[d].index(core)
            g.wait_ge(S.pf_, count(topo.mask(d, core)))
            out([T.pf[:, 0:128], T.pf[:, 128:256]], [(lane[d][i], T.pin[:, 256:384])], S.pin_)
    for d in cores:
        if core in lane[d]:
            i = lane[d].index(core)
            g.wait_ge(S.pin_, count(topo.mask(far[d][0], core)) + count(topo.mask(home[d][i], core)))
            out([T.pin[:, 128 * j:128 * j + 128] for j in range(3)], [(d, T.arr[:, 128 * i:128 * i + 128])], S["s%d_" % i])
    if sent[0]:
        g.wait_ge(S.lrel, sent[0])
